import numpy as np
import ml_dtypes


def mxq(x, axis, fmt="e4m3"):
    dtype, down = {"e4m3": (ml_dtypes.float8_e4m3fn, 7), "e5m2": (ml_dtypes.float8_e5m2, 14)}[fmt]
    v = np.moveaxis(np.asarray(x, np.float32).astype(ml_dtypes.bfloat16).astype(np.float64), axis, -1)
    blocks = v.reshape(v.shape[:-1] + (-1, 32))
    amax = np.abs(blocks).max(-1, keepdims=True)
    byte = np.maximum(np.where(amax > 0, np.frexp(amax)[1] - 1 + 127, 0) - down, 1)
    scale = np.exp2(byte - 127.0)
    codes = (blocks / scale).astype(np.float32).astype(dtype).astype(np.float64)
    return np.moveaxis((codes * scale).reshape(v.shape), -1, axis)


WIDE = False


def mx_kscale(k):
    if not WIDE:
        return np.ones(k)
    levels = np.array([10, -10, 5, -5, 0])
    if k % 512:
        return np.exp2(np.random.permutation(np.resize(levels, k // 32))).repeat(32)
    a = np.empty((k // 512, 16))
    for p in range(k // 512):
        a[p, :8] = np.random.permutation(np.resize(levels, 8))
        for g in range(8):
            far = levels[np.abs(levels - a[p, g]) >= 10]
            a[p, g + 8] = far[np.random.randint(len(far))]
    return np.exp2(a.ravel()).repeat(32)


def f64(x):
    return np.asarray(x).astype(np.float64)


def striped(idx):
    return np.tile(idx.reshape(-1, 16).T, (8, 1)).astype(np.uint16)


def unstriped(offs):
    return offs[:16].T.reshape(-1).astype(np.int64)


def pack_weight(w):
    k, n = w.shape
    w = f64(np.asarray(w, np.float32).astype(ml_dtypes.bfloat16)).reshape(k // 32, 32, n)
    amax = np.abs(w).max(1)
    byte = np.clip(np.where(amax > 0, np.frexp(amax)[1] - 1 + 127 - 7, 1), 1, 254)
    scaled = (w * np.exp2(127.0 - byte)[:, None, :]).reshape(k, n).astype(np.float32)
    words = np.ascontiguousarray(scaled.reshape(k // 512, 128, 4, n).transpose(0, 1, 3, 2)).astype(ml_dtypes.float8_e4m3fn).view(np.uint8)
    return words, np.ascontiguousarray(byte.astype(np.uint8).reshape(k // 512, 16, n))


def unpack_weight(words, scales):
    g, p, n, _ = words.shape
    vals = np.ascontiguousarray(words).view(ml_dtypes.float8_e4m3fn).astype(np.float64) * np.repeat(np.exp2(scales.astype(np.float64) - 127.0), 8, axis=1)[..., None]
    return vals.transpose(0, 1, 3, 2).reshape(g * 512, n)


def sigmoid(v):
    return 1.0 / (1.0 + np.exp(-np.maximum(v, -700.0)))


def gelu(v):
    return 0.5 * v * (1.0 + np.tanh(np.sqrt(2.0 / np.pi) * (v + 0.044715 * v**3)))


K, T, S, N = 512, 2048, 1024, 128


def setup_inputs():
    n = np.random.standard_normal
    s = mx_kscale(K)[:, None]
    packed_xT = pack_weight(n((K, T)) * s)
    return {
        "x_words": packed_xT[0],
        "x_scales": packed_xT[1],
        "res": n((N, T)).astype(np.float32),
        "w1": (n((K, N)) / np.sqrt(K) / s).astype(np.float32),
        "w2": (n((K, N)) / np.sqrt(K) / s).astype(np.float32),
        "offs": striped(np.random.permutation(T)[:S]),
    }


def reference(x_words, x_scales, res, w1, w2, offs):
    r = f64(res)[:, unstriped(offs)]
    xq = unpack_weight(x_words, x_scales)[:, unstriped(offs)]
    g = sigmoid(mxq(f64(w2), 0, "e4m3").T @ xq)
    y = gelu(mxq(f64(w1), 0, "e4m3").T @ xq)
    return r + g * (y - r)

@@ -1,0 +1,124 @@
+from contextlib import ExitStack
+
+import concourse.mybir as mybir
+
+K, T, S, N = 512, 2048, 1024, 128
+FLOPS = 2 * 2 * K * S * N
+
+F32 = mybir.dt.float32
+BF16 = mybir.dt.bfloat16
+I32 = mybir.dt.int32
+U32 = mybir.dt.uint32
+U16 = mybir.dt.uint16
+U8 = mybir.dt.uint8
+FP8X4 = mybir.dt.float8_e4m3fn_x4
+ACT = mybir.ActivationFunctionType
+ALU = mybir.AluOpType
+
+P = 128
+PACK = 4
+CHUNK = 256
+CHUNKS = S // CHUNK
+
+
+def tile_picked_highway_gelu_p_kernel(tc, x_words, x_scales, res, w1, w2, offs, out):
+    nc = tc.nc
+    with ExitStack() as ctx:
+        keep = ctx.enter_context(tc.tile_pool(name="keep", bufs=1))
+        psum = ctx.enter_context(tc.psum_pool(name="psum", bufs=1))
+
+        offsets = keep.tile([P, S // 16], U16, name="offsets")
+        nc.sync.dma_start(offsets[:], offs)
+
+        scale_table = keep.tile([P, T], U8, name="scale_table", align_bytes=64)
+        nc.vector.memset(scale_table[:].bitcast(I32), 0)
+        for q in range(4):
+            nc.scalar.dma_start(
+                out=scale_table[32 * q : 32 * q + 4, :].bitcast(I32),
+                in_=x_scales[0, 4 * q : 4 * q + 4, :].bitcast(I32),
+            )
+        warm_in = keep.tile([P, 1], F32, name="warm_in")
+        warm_out = keep.tile([P, 1], F32, name="warm_out")
+        nc.vector.memset(warm_in[:], 0.0)
+        nc.scalar.activation(out=warm_out[:], in_=warm_in[:], func=ACT.Gelu_apprx_tanh)
+
+        w2_raw = keep.tile([P, PACK, N], F32, name="w2_raw")
+        nc.sync.dma_start(out=w2_raw[:], in_=w2.rearrange("(p j) n -> p j n", j=PACK))
+        word_table = keep.tile([P, T], I32, name="word_table", align_bytes=64)
+        nc.sync.dma_start(out=word_table[:], in_=x_words[0].rearrange("p n t -> p (n t)").bitcast(I32))
+        w1_raw = keep.tile([P, PACK, N], F32, name="w1_raw")
+        nc.sync.dma_start(out=w1_raw[:], in_=w1.rearrange("(p j) n -> p j n", j=PACK))
+        res_table = keep.tile([P, T], F32, name="res_table", align_bytes=64)
+        nc.sync.dma_start(out=res_table[:], in_=res)
+
+        x_scale = keep.tile([P, S], U8, name="x_scale", align_bytes=64)
+        nc.vector.tensor_copy(out=x_scale[:], in_=scale_table[:].indirect(offsets[:]))
+
+        def quantize(raw, label):
+            grouped = keep.tile([P, N, PACK], BF16, name=label + "_grouped", align_bytes=64)
+            nc.scalar.activation(out=grouped[:], in_=raw[:].rearrange("p j n -> p n j"), func=ACT.Copy)
+            codes = keep.tile([P, N], U32, name=label + "_codes", align_bytes=64)
+            scales = keep.tile([P, N], U8, name=label + "_scales", align_bytes=64)
+            nc.vector.quantize_mx(
+                out=codes[:].bitcast(FP8X4), scales=scales[:], in_=grouped[:].rearrange("p n j -> p (n j)")
+            )
+            return codes, scales
+
+        def picked(c):
+            return offsets[:, c * CHUNK // 16 : (c + 1) * CHUNK // 16]
+
+        def product(weights, x_codes, c, label):
+            codes, scales = weights
+            acc = psum.tile([P, CHUNK], F32, name=label + "%d" % c)
+            nc.tensor.matmul_mx(
+                out=acc[:],
+                lhsT=codes[:].bitcast(FP8X4),
+                lhsT_scale=scales[:],
+                rhs=x_codes[:].bitcast(FP8X4),
+                rhs_scale=x_scale[:, c * CHUNK : (c + 1) * CHUNK],
+                start=True,
+                stop=True,
+            )
+            return acc
+
+        w2_mx = quantize(w2_raw, "w2")
+        x_codes = []
+        for c in range(CHUNKS):
+            codes = keep.tile([P, CHUNK], U32, name="x_codes%d" % c, align_bytes=64)
+            nc.vector.tensor_copy(out=codes[:], in_=word_table[:].bitcast(U32).indirect(picked(c)))
+            x_codes.append(codes)
+            if c == 1:
+                w1_mx = quantize(w1_raw, "w1")
+
+        carry, value = [], []
+        for c in range(CHUNKS):
+            gate_sum = product(w2_mx, x_codes[c], c, "gate_sum")
+            value_sum = product(w1_mx, x_codes[c], c, "value_sum")
+            th = keep.tile([P, CHUNK], F32, name="th%d" % c)
+            nc.scalar.activation(out=th[:], in_=gate_sum[:], func=ACT.Tanh, scale=0.5)
+            cr = keep.tile([P, CHUNK], F32, name="carry%d" % c)
+            nc.scalar.activation(out=cr[:], in_=th[:], func=ACT.Copy, scale=-0.5, bias=0.5)
+            y = keep.tile([P, CHUNK], F32, name="value%d" % c)
+            nc.scalar.activation(out=y[:], in_=value_sum[:], func=ACT.Gelu_apprx_tanh)
+            carry.append(cr)
+            value.append(y)
+
+        def finish(c, passed, gated):
+            result = keep.tile([P, CHUNK], F32, name="result%d" % c)
+            nc.vector.tensor_tensor(out=result[:], in0=passed[:], in1=gated[:], op=ALU.subtract)
+            nc.sync.dma_start(out=out[:, c * CHUNK : (c + 1) * CHUNK], in_=result[:])
+
+        pending = None
+        for c in range(CHUNKS):
+            gated = keep.tile([P, CHUNK], F32, name="gated%d" % c)
+            nc.vector.scalar_tensor_tensor(
+                out=gated[:], in0=carry[c][:], scalar=-1.0, in1=value[c][:], op0=ALU.add, op1=ALU.mult
+            )
+            passed = keep.tile([P, CHUNK], F32, name="passed%d" % c)
+            nc.vector.tensor_tensor(
+                out=passed[:], in0=res_table[:].indirect(picked(c)), in1=carry[c][:], op=ALU.mult
+            )
+            if pending is not None:
+                finish(*pending)
+            pending = (c, passed, gated)
+        finish(*pending)

@@ -17,8 +17,10 @@ ALU = mybir.AluOpType
 
 P = 128
 PACK = 4
-CHUNK = 256
+CHUNK = 512
 CHUNKS = S // CHUNK
+EDGES = (0, 320, 640, 896, 1024)
+PIECES = len(EDGES) - 1
 
 
 def tile_picked_highway_gelu_p_kernel(tc, x_words, x_scales, res, w1, w2, offs, out):
@@ -32,22 +34,22 @@ def tile_picked_highway_gelu_p_kernel(tc, x_words, x_scales, res, w1, w2, offs, 
 
         scale_table = keep.tile([P, T], U8, name="scale_table", align_bytes=64)
         nc.vector.memset(scale_table[:].bitcast(I32), 0)
-        for q in range(4):
-            nc.scalar.dma_start(
-                out=scale_table[32 * q : 32 * q + 4, :].bitcast(I32),
-                in_=x_scales[0, 4 * q : 4 * q + 4, :].bitcast(I32),
-            )
         warm_in = keep.tile([P, 1], F32, name="warm_in")
         warm_out = keep.tile([P, 1], F32, name="warm_out")
         nc.vector.memset(warm_in[:], 0.0)
         nc.scalar.activation(out=warm_out[:], in_=warm_in[:], func=ACT.Gelu_apprx_tanh)
 
-        w2_raw = keep.tile([P, PACK, N], F32, name="w2_raw")
-        nc.sync.dma_start(out=w2_raw[:], in_=w2.rearrange("(p j) n -> p j n", j=PACK))
-        word_table = keep.tile([P, T], I32, name="word_table", align_bytes=64)
-        nc.sync.dma_start(out=word_table[:], in_=x_words[0].rearrange("p n t -> p (n t)").bitcast(I32))
         w1_raw = keep.tile([P, PACK, N], F32, name="w1_raw")
         nc.sync.dma_start(out=w1_raw[:], in_=w1.rearrange("(p j) n -> p j n", j=PACK))
+        for q in range(4):
+            nc.sync.dma_start(
+                out=scale_table[32 * q : 32 * q + 4, :].bitcast(I32),
+                in_=x_scales[0, 4 * q : 4 * q + 4, :].bitcast(I32),
+            )
+        word_table = keep.tile([P, T], I32, name="word_table", align_bytes=64)
+        nc.sync.dma_start(out=word_table[:], in_=x_words[0].rearrange("p n t -> p (n t)").bitcast(I32))
+        w2_raw = keep.tile([P, PACK, N], F32, name="w2_raw")
+        nc.sync.dma_start(out=w2_raw[:], in_=w2.rearrange("(p j) n -> p j n", j=PACK))
         res_table = keep.tile([P, T], F32, name="res_table", align_bytes=64)
         nc.sync.dma_start(out=res_table[:], in_=res)
 
@@ -81,44 +83,43 @@ def tile_picked_highway_gelu_p_kernel(tc, x_words, x_scales, res, w1, w2, offs, 
             )
             return acc
 
-        w2_mx = quantize(w2_raw, "w2")
+        w1_mx = quantize(w1_raw, "w1")
         x_codes = []
         for c in range(CHUNKS):
             codes = keep.tile([P, CHUNK], U32, name="x_codes%d" % c, align_bytes=64)
             nc.vector.tensor_copy(out=codes[:], in_=word_table[:].bitcast(U32).indirect(picked(c)))
             x_codes.append(codes)
-            if c == 1:
-                w1_mx = quantize(w1_raw, "w1")
+            if c == 0:
+                w2_mx = quantize(w2_raw, "w2")
 
-        carry, value = [], []
+        passing = keep.tile([P, S], F32, name="passing")
         for c in range(CHUNKS):
-            gate_sum = product(w2_mx, x_codes[c], c, "gate_sum")
+            nc.vector.tensor_copy(out=passing[:, c * CHUNK : (c + 1) * CHUNK], in_=res_table[:].indirect(picked(c)))
+
+        th = keep.tile([P, S], F32, name="th")
+        value = keep.tile([P, S], F32, name="value")
+        for c in range(CHUNKS):
+            cols = slice(c * CHUNK, (c + 1) * CHUNK)
             value_sum = product(w1_mx, x_codes[c], c, "value_sum")
-            th = keep.tile([P, CHUNK], F32, name="th%d" % c)
-            nc.scalar.activation(out=th[:], in_=gate_sum[:], func=ACT.Tanh, scale=0.5)
-            cr = keep.tile([P, CHUNK], F32, name="carry%d" % c)
-            nc.scalar.activation(out=cr[:], in_=th[:], func=ACT.Copy, scale=-0.5, bias=0.5)
-            y = keep.tile([P, CHUNK], F32, name="value%d" % c)
-            nc.scalar.activation(out=y[:], in_=value_sum[:], func=ACT.Gelu_apprx_tanh)
-            carry.append(cr)
-            value.append(y)
+            gate_sum = product(w2_mx, x_codes[c], c, "gate_sum")
+            nc.scalar.activation(out=value[:, cols], in_=value_sum[:], func=ACT.Gelu_apprx_tanh)
+            nc.scalar.activation(out=th[:, cols], in_=gate_sum[:], func=ACT.Tanh, scale=0.5)
 
-        def finish(c, passed, gated):
-            result = keep.tile([P, CHUNK], F32, name="result%d" % c)
-            nc.vector.tensor_tensor(out=result[:], in0=passed[:], in1=gated[:], op=ALU.subtract)
-            nc.sync.dma_start(out=out[:, c * CHUNK : (c + 1) * CHUNK], in_=result[:])
-
-        pending = None
-        for c in range(CHUNKS):
-            gated = keep.tile([P, CHUNK], F32, name="gated%d" % c)
-            nc.vector.scalar_tensor_tensor(
-                out=gated[:], in0=carry[c][:], scalar=-1.0, in1=value[c][:], op0=ALU.add, op1=ALU.mult
-            )
-            passed = keep.tile([P, CHUNK], F32, name="passed%d" % c)
-            nc.vector.tensor_tensor(
-                out=passed[:], in0=res_table[:].indirect(picked(c)), in1=carry[c][:], op=ALU.mult
-            )
-            if pending is not None:
-                finish(*pending)
-            pending = (c, passed, gated)
-        finish(*pending)
+        diff = keep.tile([P, S], F32, name="diff")
+        gated = keep.tile([P, S], F32, name="gated")
+        result = keep.tile([P, S], F32, name="result")
+        for step in range(PIECES + 2):
+            if step < PIECES:
+                cols = slice(EDGES[step], EDGES[step + 1])
+                nc.vector.tensor_tensor(out=diff[:, cols], in0=value[:, cols], in1=passing[:, cols], op=ALU.subtract)
+            if 1 <= step <= PIECES:
+                cols = slice(EDGES[step - 1], EDGES[step])
+                nc.vector.scalar_tensor_tensor(
+                    out=gated[:, cols], in0=th[:, cols], scalar=1.0, in1=diff[:, cols], op0=ALU.add, op1=ALU.mult
+                )
+            if step >= 2:
+                cols = slice(EDGES[step - 2], EDGES[step - 1])
+                nc.vector.scalar_tensor_tensor(
+                    out=result[:, cols], in0=gated[:, cols], scalar=0.5, in1=passing[:, cols], op0=ALU.mult, op1=ALU.add
+                )
+                nc.sync.dma_start(out=out[:, cols], in_=result[:, cols])

@@ -17,7 +17,7 @@ ALU = mybir.AluOpType
 
 P = 128
 PACK = 4
-CHUNK = 512
+CHUNK = 256
 CHUNKS = S // CHUNK
 EDGES = (0, 320, 640, 896, 1024)
 PIECES = len(EDGES) - 1
@@ -89,21 +89,23 @@ def tile_picked_highway_gelu_p_kernel(tc, x_words, x_scales, res, w1, w2, offs, 
             codes = keep.tile([P, CHUNK], U32, name="x_codes%d" % c, align_bytes=64)
             nc.vector.tensor_copy(out=codes[:], in_=word_table[:].bitcast(U32).indirect(picked(c)))
             x_codes.append(codes)
-            if c == 0:
+            if c == 1:
                 w2_mx = quantize(w2_raw, "w2")
 
         passing = keep.tile([P, S], F32, name="passing")
-        for c in range(CHUNKS):
-            nc.vector.tensor_copy(out=passing[:, c * CHUNK : (c + 1) * CHUNK], in_=res_table[:].indirect(picked(c)))
+        for a, b in ((0, EDGES[2]), (EDGES[2], S)):
+            nc.vector.tensor_copy(out=passing[:, a:b], in_=res_table[:].indirect(offsets[:, a // 16 : b // 16]))
 
         th = keep.tile([P, S], F32, name="th")
         value = keep.tile([P, S], F32, name="value")
+        gate = keep.tile([P, S], F32, name="gate")
         for c in range(CHUNKS):
             cols = slice(c * CHUNK, (c + 1) * CHUNK)
             value_sum = product(w1_mx, x_codes[c], c, "value_sum")
             gate_sum = product(w2_mx, x_codes[c], c, "gate_sum")
             nc.scalar.activation(out=value[:, cols], in_=value_sum[:], func=ACT.Gelu_apprx_tanh)
             nc.scalar.activation(out=th[:, cols], in_=gate_sum[:], func=ACT.Tanh, scale=0.5)
+            nc.scalar.activation(out=gate[:, cols], in_=th[:, cols], func=ACT.Copy, scale=0.5, bias=0.5)
 
         diff = keep.tile([P, S], F32, name="diff")
         gated = keep.tile([P, S], F32, name="gated")
@@ -114,12 +116,8 @@ def tile_picked_highway_gelu_p_kernel(tc, x_words, x_scales, res, w1, w2, offs, 
                 nc.vector.tensor_tensor(out=diff[:, cols], in0=value[:, cols], in1=passing[:, cols], op=ALU.subtract)
             if 1 <= step <= PIECES:
                 cols = slice(EDGES[step - 1], EDGES[step])
-                nc.vector.scalar_tensor_tensor(
-                    out=gated[:, cols], in0=th[:, cols], scalar=1.0, in1=diff[:, cols], op0=ALU.add, op1=ALU.mult
-                )
+                nc.vector.tensor_tensor(out=gated[:, cols], in0=gate[:, cols], in1=diff[:, cols], op=ALU.mult)
             if step >= 2:
                 cols = slice(EDGES[step - 2], EDGES[step - 1])
-                nc.vector.scalar_tensor_tensor(
-                    out=result[:, cols], in0=gated[:, cols], scalar=0.5, in1=passing[:, cols], op0=ALU.mult, op1=ALU.add
-                )
+                nc.vector.tensor_tensor(out=result[:, cols], in0=gated[:, cols], in1=passing[:, cols], op=ALU.add)
                 nc.sync.dma_start(out=out[:, cols], in_=result[:, cols])

@@ -19,8 +19,6 @@ P = 128
 PACK = 4
 CHUNK = 256
 CHUNKS = S // CHUNK
-EDGES = (0, 320, 640, 896, 1024)
-PIECES = len(EDGES) - 1
 
 
 def tile_picked_highway_gelu_p_kernel(tc, x_words, x_scales, res, w1, w2, offs, out):
@@ -39,43 +37,41 @@ def tile_picked_highway_gelu_p_kernel(tc, x_words, x_scales, res, w1, w2, offs, 
         nc.vector.memset(warm_in[:], 0.0)
         nc.scalar.activation(out=warm_out[:], in_=warm_in[:], func=ACT.Gelu_apprx_tanh)
 
-        w1_raw = keep.tile([P, PACK, N], F32, name="w1_raw")
-        nc.sync.dma_start(out=w1_raw[:], in_=w1.rearrange("(p j) n -> p j n", j=PACK))
-        for q in range(4):
-            nc.sync.dma_start(
-                out=scale_table[32 * q : 32 * q + 4, :].bitcast(I32),
-                in_=x_scales[0, 4 * q : 4 * q + 4, :].bitcast(I32),
-            )
-        word_table = keep.tile([P, T], I32, name="word_table", align_bytes=64)
-        nc.sync.dma_start(out=word_table[:], in_=x_words[0].rearrange("p n t -> p (n t)").bitcast(I32))
         w2_raw = keep.tile([P, PACK, N], F32, name="w2_raw")
         nc.sync.dma_start(out=w2_raw[:], in_=w2.rearrange("(p j) n -> p j n", j=PACK))
+        for i in range(4):
+            nc.sync.dma_start(
+                out=scale_table[i:P:32, :].bitcast(I32),
+                in_=x_scales[0, i:16:4, :].bitcast(I32),
+            )
+        w1_raw = keep.tile([P, PACK, N], F32, name="w1_raw")
+        nc.sync.dma_start(out=w1_raw[:], in_=w1.rearrange("(p j) n -> p j n", j=PACK))
+        word_table = keep.tile([P, T], I32, name="word_table", align_bytes=64)
+        nc.sync.dma_start(out=word_table[:], in_=x_words[0].rearrange("p n t -> p (n t)").bitcast(I32))
         res_table = keep.tile([P, T], F32, name="res_table", align_bytes=64)
         nc.sync.dma_start(out=res_table[:], in_=res)
 
         x_scale = keep.tile([P, S], U8, name="x_scale", align_bytes=64)
         nc.vector.tensor_copy(out=x_scale[:], in_=scale_table[:].indirect(offsets[:]))
 
-        def quantize(raw, label):
-            grouped = keep.tile([P, N, PACK], BF16, name=label + "_grouped", align_bytes=64)
-            nc.scalar.activation(out=grouped[:], in_=raw[:].rearrange("p j n -> p n j"), func=ACT.Copy)
-            codes = keep.tile([P, N], U32, name=label + "_codes", align_bytes=64)
-            scales = keep.tile([P, N], U8, name=label + "_scales", align_bytes=64)
-            nc.vector.quantize_mx(
-                out=codes[:].bitcast(FP8X4), scales=scales[:], in_=grouped[:].rearrange("p n j -> p (n j)")
-            )
-            return codes, scales
-
-        def picked(c):
-            return offsets[:, c * CHUNK // 16 : (c + 1) * CHUNK // 16]
+        grouped = keep.tile([P, 2, N, PACK], BF16, name="grouped", align_bytes=64)
+        for slot, raw in enumerate((w2_raw, w1_raw)):
+            nc.scalar.activation(out=grouped[:, slot], in_=raw[:].rearrange("p j n -> p n j"), func=ACT.Copy)
+        w_codes = keep.tile([P, 2 * N], U32, name="w_codes", align_bytes=64)
+        w_scales = keep.tile([P, 2 * N], U8, name="w_scales", align_bytes=64)
+        nc.vector.quantize_mx(
+            out=w_codes[:].bitcast(FP8X4), scales=w_scales[:], in_=grouped[:].rearrange("p s n j -> p (s n j)")
+        )
+        w2_mx = (w_codes[:, :N], w_scales[:, :N])
+        w1_mx = (w_codes[:, N:], w_scales[:, N:])
 
         def product(weights, x_codes, c, label):
             codes, scales = weights
             acc = psum.tile([P, CHUNK], F32, name=label + "%d" % c)
             nc.tensor.matmul_mx(
                 out=acc[:],
-                lhsT=codes[:].bitcast(FP8X4),
-                lhsT_scale=scales[:],
+                lhsT=codes.bitcast(FP8X4),
+                lhsT_scale=scales,
                 rhs=x_codes[:].bitcast(FP8X4),
                 rhs_scale=x_scale[:, c * CHUNK : (c + 1) * CHUNK],
                 start=True,
@@ -83,41 +79,68 @@ def tile_picked_highway_gelu_p_kernel(tc, x_words, x_scales, res, w1, w2, offs, 
             )
             return acc
 
-        w1_mx = quantize(w1_raw, "w1")
         x_codes = []
         for c in range(CHUNKS):
             codes = keep.tile([P, CHUNK], U32, name="x_codes%d" % c, align_bytes=64)
-            nc.vector.tensor_copy(out=codes[:], in_=word_table[:].bitcast(U32).indirect(picked(c)))
+            picked = offsets[:, c * CHUNK // 16 : (c + 1) * CHUNK // 16]
+            nc.vector.tensor_copy(out=codes[:], in_=word_table[:].bitcast(U32).indirect(picked))
             x_codes.append(codes)
-            if c == 1:
-                w2_mx = quantize(w2_raw, "w2")
 
         passing = keep.tile([P, S], F32, name="passing")
-        for a, b in ((0, EDGES[2]), (EDGES[2], S)):
+        for a, b in ((0, S // 2), (S // 2, S)):
             nc.vector.tensor_copy(out=passing[:, a:b], in_=res_table[:].indirect(offsets[:, a // 16 : b // 16]))
 
         th = keep.tile([P, S], F32, name="th")
         value = keep.tile([P, S], F32, name="value")
-        gate = keep.tile([P, S], F32, name="gate")
+        gate = keep.tile([P, S // 2], F32, name="gate")
+        gated = keep.tile([P, S], F32, name="gated")
         for c in range(CHUNKS):
             cols = slice(c * CHUNK, (c + 1) * CHUNK)
-            value_sum = product(w1_mx, x_codes[c], c, "value_sum")
             gate_sum = product(w2_mx, x_codes[c], c, "gate_sum")
-            nc.scalar.activation(out=value[:, cols], in_=value_sum[:], func=ACT.Gelu_apprx_tanh)
-            nc.scalar.activation(out=th[:, cols], in_=gate_sum[:], func=ACT.Tanh, scale=0.5)
-            nc.scalar.activation(out=gate[:, cols], in_=th[:, cols], func=ACT.Copy, scale=0.5, bias=0.5)
+            value_sum = product(w1_mx, x_codes[c], c, "value_sum")
+            if c < CHUNKS // 2:
+                nc.scalar.activation(out=th[:, cols], in_=gate_sum[:], func=ACT.Tanh, scale=0.5)
+                nc.scalar.activation(out=gate[:, cols], in_=th[:, cols], func=ACT.Copy, scale=0.5, bias=0.5)
+                nc.scalar.activation(out=value[:, cols], in_=value_sum[:], func=ACT.Gelu_apprx_tanh)
+                nc.gpsimd.tensor_tensor(out=gated[:, cols], in0=gate[:, cols], in1=value[:, cols], op=ALU.mult)
+            else:
+                nc.scalar.activation(out=value[:, cols], in_=value_sum[:], func=ACT.Gelu_apprx_tanh)
+                nc.scalar.activation(out=th[:, cols], in_=gate_sum[:], func=ACT.Tanh, scale=0.5)
 
-        diff = keep.tile([P, S], F32, name="diff")
-        gated = keep.tile([P, S], F32, name="gated")
+        mixed = keep.tile([P, S], F32, name="mixed")
         result = keep.tile([P, S], F32, name="result")
-        for step in range(PIECES + 2):
-            if step < PIECES:
-                cols = slice(EDGES[step], EDGES[step + 1])
-                nc.vector.tensor_tensor(out=diff[:, cols], in0=value[:, cols], in1=passing[:, cols], op=ALU.subtract)
-            if 1 <= step <= PIECES:
-                cols = slice(EDGES[step - 1], EDGES[step])
-                nc.vector.tensor_tensor(out=gated[:, cols], in0=gate[:, cols], in1=diff[:, cols], op=ALU.mult)
-            if step >= 2:
-                cols = slice(EDGES[step - 2], EDGES[step - 1])
-                nc.vector.tensor_tensor(out=result[:, cols], in0=gated[:, cols], in1=passing[:, cols], op=ALU.add)
-                nc.sync.dma_start(out=out[:, cols], in_=result[:, cols])
+        pieces = [slice(0, 256), slice(256, 512), slice(512, 832), slice(832, 1024)]
+
+        def carry(cols):
+            nc.vector.scalar_tensor_tensor(
+                out=mixed[:, cols], in0=gate[:, cols], scalar=-1.0, in1=passing[:, cols], op0=ALU.add, op1=ALU.mult
+            )
+
+        def join(cols):
+            nc.vector.tensor_tensor(out=result[:, cols], in0=gated[:, cols], in1=mixed[:, cols], op=ALU.subtract)
+            nc.sync.dma_start(out=out[:, cols], in_=result[:, cols])
+
+        def differ(cols):
+            nc.vector.tensor_tensor(out=mixed[:, cols], in0=value[:, cols], in1=passing[:, cols], op=ALU.subtract)
+
+        def weigh(cols):
+            nc.vector.scalar_tensor_tensor(
+                out=gated[:, cols], in0=th[:, cols], scalar=1.0, in1=mixed[:, cols], op0=ALU.add, op1=ALU.mult
+            )
+
+        def add_back(cols):
+            nc.vector.scalar_tensor_tensor(
+                out=result[:, cols], in0=gated[:, cols], scalar=0.5, in1=passing[:, cols], op0=ALU.mult, op1=ALU.add
+            )
+            nc.sync.dma_start(out=out[:, cols], in_=result[:, cols])
+
+        carry(pieces[0])
+        differ(pieces[2])
+        carry(pieces[1])
+        differ(pieces[3])
+        join(pieces[0])
+        weigh(pieces[2])
+        weigh(pieces[3])
+        join(pieces[1])
+        add_back(pieces[2])
+        add_back(pieces[3])

@@ -86,61 +86,44 @@ def tile_picked_highway_gelu_p_kernel(tc, x_words, x_scales, res, w1, w2, offs, 
             nc.vector.tensor_copy(out=codes[:], in_=word_table[:].bitcast(U32).indirect(picked))
             x_codes.append(codes)
 
-        passing = keep.tile([P, S], F32, name="passing")
-        for a, b in ((0, S // 2), (S // 2, S)):
-            nc.vector.tensor_copy(out=passing[:, a:b], in_=res_table[:].indirect(offsets[:, a // 16 : b // 16]))
-
         th = keep.tile([P, S], F32, name="th")
         value = keep.tile([P, S], F32, name="value")
-        gate = keep.tile([P, S // 2], F32, name="gate")
-        gated = keep.tile([P, S], F32, name="gated")
+        gate_sums = []
         for c in range(CHUNKS):
             cols = slice(c * CHUNK, (c + 1) * CHUNK)
-            gate_sum = product(w2_mx, x_codes[c], c, "gate_sum")
             value_sum = product(w1_mx, x_codes[c], c, "value_sum")
-            if c < CHUNKS // 2:
-                nc.scalar.activation(out=th[:, cols], in_=gate_sum[:], func=ACT.Tanh, scale=0.5)
-                nc.scalar.activation(out=gate[:, cols], in_=th[:, cols], func=ACT.Copy, scale=0.5, bias=0.5)
-                nc.scalar.activation(out=value[:, cols], in_=value_sum[:], func=ACT.Gelu_apprx_tanh)
-                nc.gpsimd.tensor_tensor(out=gated[:, cols], in0=gate[:, cols], in1=value[:, cols], op=ALU.mult)
-            else:
-                nc.scalar.activation(out=value[:, cols], in_=value_sum[:], func=ACT.Gelu_apprx_tanh)
-                nc.scalar.activation(out=th[:, cols], in_=gate_sum[:], func=ACT.Tanh, scale=0.5)
+            gate_sums.append(product(w2_mx, x_codes[c], c, "gate_sum"))
+            nc.scalar.activation(out=value[:, cols], in_=value_sum[:], func=ACT.Gelu_apprx_tanh)
+            nc.scalar.activation(out=th[:, cols], in_=gate_sums[c][:], func=ACT.Tanh, scale=0.5)
 
-        mixed = keep.tile([P, S], F32, name="mixed")
+        diff = keep.tile([P, S], F32, name="diff")
+        weighed = keep.tile([P, S], F32, name="weighed")
         result = keep.tile([P, S], F32, name="result")
-        pieces = [slice(0, 256), slice(256, 512), slice(512, 832), slice(832, 1024)]
 
-        def carry(cols):
-            nc.vector.scalar_tensor_tensor(
-                out=mixed[:, cols], in0=gate[:, cols], scalar=-1.0, in1=passing[:, cols], op0=ALU.add, op1=ALU.mult
+        def differ(c):
+            cols = slice(c * CHUNK, (c + 1) * CHUNK)
+            picked = offsets[:, c * CHUNK // 16 : (c + 1) * CHUNK // 16]
+            nc.vector.tensor_tensor(
+                out=diff[:, cols], in0=res_table[:].indirect(picked), in1=value[:, cols], op=ALU.subtract
             )
 
-        def join(cols):
-            nc.vector.tensor_tensor(out=result[:, cols], in0=gated[:, cols], in1=mixed[:, cols], op=ALU.subtract)
-            nc.sync.dma_start(out=out[:, cols], in_=result[:, cols])
-
-        def differ(cols):
-            nc.vector.tensor_tensor(out=mixed[:, cols], in0=value[:, cols], in1=passing[:, cols], op=ALU.subtract)
-
-        def weigh(cols):
+        def weigh(c):
+            cols = slice(c * CHUNK, (c + 1) * CHUNK)
             nc.vector.scalar_tensor_tensor(
-                out=gated[:, cols], in0=th[:, cols], scalar=1.0, in1=mixed[:, cols], op0=ALU.add, op1=ALU.mult
+                out=weighed[:, cols], in0=th[:, cols], scalar=-1.0, in1=diff[:, cols], op0=ALU.add, op1=ALU.mult
             )
 
-        def add_back(cols):
+        def add_back(c):
+            cols = slice(c * CHUNK, (c + 1) * CHUNK)
             nc.vector.scalar_tensor_tensor(
-                out=result[:, cols], in0=gated[:, cols], scalar=0.5, in1=passing[:, cols], op0=ALU.mult, op1=ALU.add
+                out=result[:, cols], in0=weighed[:, cols], scalar=-0.5, in1=value[:, cols], op0=ALU.mult, op1=ALU.add
             )
             nc.sync.dma_start(out=out[:, cols], in_=result[:, cols])
 
-        carry(pieces[0])
-        differ(pieces[2])
-        carry(pieces[1])
-        differ(pieces[3])
-        join(pieces[0])
-        weigh(pieces[2])
-        weigh(pieces[3])
-        join(pieces[1])
-        add_back(pieces[2])
-        add_back(pieces[3])
+        for step in range(CHUNKS + 2):
+            if step < CHUNKS:
+                differ(step)
+            if 1 <= step <= CHUNKS:
+                weigh(step - 1)
+            if step >= 2:
+                add_back(step - 2)

@@ -1,6 +1,7 @@
 from contextlib import ExitStack
 
 import concourse.mybir as mybir
+from concourse.masks import make_identity
 
 K, T, S, N = 512, 2048, 1024, 128
 FLOPS = 2 * 2 * K * S * N
@@ -19,6 +20,8 @@ P = 128
 PACK = 4
 CHUNK = 256
 CHUNKS = S // CHUNK
+BLOCKS = CHUNK // P
+SUMMED_ON_TENSOR = 2
 
 
 def tile_picked_highway_gelu_p_kernel(tc, x_words, x_scales, res, w1, w2, offs, out):
@@ -32,10 +35,13 @@ def tile_picked_highway_gelu_p_kernel(tc, x_words, x_scales, res, w1, w2, offs, 
 
         scale_table = keep.tile([P, T], U8, name="scale_table", align_bytes=64)
         nc.vector.memset(scale_table[:].bitcast(I32), 0)
-        warm_in = keep.tile([P, 1], F32, name="warm_in")
+        warm_in = keep.tile([P, 1], F32, name="warm_in", tag="identity")
         warm_out = keep.tile([P, 1], F32, name="warm_out")
         nc.vector.memset(warm_in[:], 0.0)
         nc.scalar.activation(out=warm_out[:], in_=warm_in[:], func=ACT.Gelu_apprx_tanh)
+
+        identity = keep.tile([P, P], F32, name="identity", tag="identity")
+        make_identity(nc, identity[:])
 
         w2_raw = keep.tile([P, PACK, N], F32, name="w2_raw")
         nc.sync.dma_start(out=w2_raw[:], in_=w2.rearrange("(p j) n -> p j n", j=PACK))
@@ -65,9 +71,9 @@ def tile_picked_highway_gelu_p_kernel(tc, x_words, x_scales, res, w1, w2, offs, 
         w2_mx = (w_codes[:, :N], w_scales[:, :N])
         w1_mx = (w_codes[:, N:], w_scales[:, N:])
 
-        def product(weights, x_codes, c, label):
+        def product(weights, x_codes, c, label, bank):
             codes, scales = weights
-            acc = psum.tile([P, CHUNK], F32, name=label + "%d" % c)
+            acc = psum.tile([P, CHUNK], F32, name=label + "%d" % c, tag="bank%d" % bank)
             nc.tensor.matmul_mx(
                 out=acc[:],
                 lhsT=codes.bitcast(FP8X4),
@@ -91,10 +97,10 @@ def tile_picked_highway_gelu_p_kernel(tc, x_words, x_scales, res, w1, w2, offs, 
         gate_sums = []
         for c in range(CHUNKS):
             cols = slice(c * CHUNK, (c + 1) * CHUNK)
-            value_sum = product(w1_mx, x_codes[c], c, "value_sum")
-            gate_sums.append(product(w2_mx, x_codes[c], c, "gate_sum"))
+            value_sum = product(w1_mx, x_codes[c], c, "value_sum", 2 * c)
+            gate_sums.append(product(w2_mx, x_codes[c], c, "gate_sum", 2 * c + 1))
             nc.scalar.activation(out=value[:, cols], in_=value_sum[:], func=ACT.Gelu_apprx_tanh)
-            nc.scalar.activation(out=th[:, cols], in_=gate_sums[c][:], func=ACT.Tanh, scale=0.5)
+            nc.scalar.activation(out=th[:, cols], in_=gate_sums[c][:], func=ACT.Tanh, scale=-0.5)
 
         diff = keep.tile([P, S], F32, name="diff")
         weighed = keep.tile([P, S], F32, name="weighed")
@@ -110,20 +116,59 @@ def tile_picked_highway_gelu_p_kernel(tc, x_words, x_scales, res, w1, w2, offs, 
         def weigh(c):
             cols = slice(c * CHUNK, (c + 1) * CHUNK)
             nc.vector.scalar_tensor_tensor(
-                out=weighed[:, cols], in0=th[:, cols], scalar=-1.0, in1=diff[:, cols], op0=ALU.add, op1=ALU.mult
+                out=weighed[:, cols], in0=th[:, cols], scalar=1.0, in1=diff[:, cols], op0=ALU.add, op1=ALU.mult
             )
 
         def add_back(c):
             cols = slice(c * CHUNK, (c + 1) * CHUNK)
             nc.vector.scalar_tensor_tensor(
-                out=result[:, cols], in0=weighed[:, cols], scalar=-0.5, in1=value[:, cols], op0=ALU.mult, op1=ALU.add
+                out=result[:, cols], in0=weighed[:, cols], scalar=0.5, in1=value[:, cols], op0=ALU.mult, op1=ALU.add
             )
             nc.sync.dma_start(out=out[:, cols], in_=result[:, cols])
 
-        for step in range(CHUNKS + 2):
-            if step < CHUNKS:
-                differ(step)
-            if 1 <= step <= CHUNKS:
-                weigh(step - 1)
-            if step >= 2:
-                add_back(step - 2)
+        turned = keep.tile([P, SUMMED_ON_TENSOR * CHUNK], F32, name="turned")
+        sums = []
+
+        def open_sums(c):
+            for b in range(c * BLOCKS, (c + 1) * BLOCKS):
+                acc = psum.tile([P, P], F32, name="sum%d" % b, tag="bank%d" % b)
+                for first in (True, False):
+                    nc.tensor.matmul(
+                        acc[:], lhsT=value[:, b * P : (b + 1) * P], rhs=identity[:],
+                        is_transpose=True, start=first, stop=False,
+                    )
+                sums.append(acc)
+
+        def close_sums(c):
+            for b in range(c * BLOCKS, (c + 1) * BLOCKS):
+                nc.tensor.matmul(
+                    sums[b][:], lhsT=weighed[:, b * P : (b + 1) * P], rhs=identity[:],
+                    is_transpose=True, start=False, stop=True,
+                )
+                nc.scalar.activation(out=turned[:, b * P : (b + 1) * P], in_=sums[b][:], func=ACT.Copy)
+
+        def turn_back(c):
+            cols = slice(c * CHUNK, (c + 1) * CHUNK)
+            back = psum.tile([P, CHUNK], F32, name="back%d" % c, tag="bank%d" % (SUMMED_ON_TENSOR * BLOCKS + c))
+            for i in range(BLOCKS):
+                b = c * BLOCKS + i
+                nc.tensor.transpose(back[:, i * P : (i + 1) * P], turned[:, b * P : (b + 1) * P], identity[:])
+            nc.scalar.activation(out=result[:, cols], in_=back[:], func=ACT.Copy, scale=0.5)
+            nc.scalar.dma_start(out=out[:, cols], in_=result[:, cols])
+
+        differ(0)
+        differ(1)
+        weigh(0)
+        open_sums(0)
+        close_sums(0)
+        weigh(1)
+        open_sums(1)
+        turn_back(0)
+        close_sums(1)
+        turn_back(1)
+        differ(2)
+        differ(3)
+        weigh(2)
+        weigh(3)
+        add_back(2)
+        add_back(3)

@@ -35,13 +35,9 @@ def tile_picked_highway_gelu_p_kernel(tc, x_words, x_scales, res, w1, w2, offs, 
 
         scale_table = keep.tile([P, T], U8, name="scale_table", align_bytes=64)
         nc.vector.memset(scale_table[:].bitcast(I32), 0)
-        warm_in = keep.tile([P, 1], F32, name="warm_in", tag="identity")
-        warm_out = keep.tile([P, 1], F32, name="warm_out")
-        nc.vector.memset(warm_in[:], 0.0)
-        nc.scalar.activation(out=warm_out[:], in_=warm_in[:], func=ACT.Gelu_apprx_tanh)
-
-        identity = keep.tile([P, P], F32, name="identity", tag="identity")
-        make_identity(nc, identity[:])
+        identity = keep.tile([P, P], F32, name="identity")
+        nc.vector.memset(identity[:], 0.0)
+        make_identity(nc, identity[:], nomemset=True)
 
         w2_raw = keep.tile([P, PACK, N], F32, name="w2_raw")
         nc.sync.dma_start(out=w2_raw[:], in_=w2.rearrange("(p j) n -> p j n", j=PACK))
@@ -62,7 +58,7 @@ def tile_picked_highway_gelu_p_kernel(tc, x_words, x_scales, res, w1, w2, offs, 
 
         grouped = keep.tile([P, 2, N, PACK], BF16, name="grouped", align_bytes=64)
         for slot, raw in enumerate((w2_raw, w1_raw)):
-            nc.scalar.activation(out=grouped[:, slot], in_=raw[:].rearrange("p j n -> p n j"), func=ACT.Copy)
+            nc.scalar.copy(out=grouped[:, slot], in_=raw[:].rearrange("p j n -> p n j"))
         w_codes = keep.tile([P, 2 * N], U32, name="w_codes", align_bytes=64)
         w_scales = keep.tile([P, 2 * N], U8, name="w_scales", align_bytes=64)
         nc.vector.quantize_mx(

@@ -20,8 +20,8 @@ P = 128
 PACK = 4
 CHUNK = 256
 CHUNKS = S // CHUNK
-BLOCKS = CHUNK // P
-SUMMED_ON_TENSOR = 2
+EARLY_WIDTHS = (256, 256,)
+LATE_WIDTHS = (256, 128, 128,)
 
 
 def tile_picked_highway_gelu_p_kernel(tc, x_words, x_scales, res, w1, w2, offs, out):
@@ -101,70 +101,67 @@ def tile_picked_highway_gelu_p_kernel(tc, x_words, x_scales, res, w1, w2, offs, 
         diff = keep.tile([P, S], F32, name="diff")
         weighed = keep.tile([P, S], F32, name="weighed")
         result = keep.tile([P, S], F32, name="result")
+        turned = keep.tile([P, sum(EARLY_WIDTHS)], F32, name="turned")
+        pieces = []
+        for width in EARLY_WIDTHS + LATE_WIDTHS:
+            start = pieces[-1].stop if pieces else 0
+            pieces.append(slice(start, start + width))
 
         def differ(c):
             cols = slice(c * CHUNK, (c + 1) * CHUNK)
-            picked = offsets[:, c * CHUNK // 16 : (c + 1) * CHUNK // 16]
+            picked = offsets[:, cols.start // 16 : cols.stop // 16]
             nc.vector.tensor_tensor(
                 out=diff[:, cols], in0=res_table[:].indirect(picked), in1=value[:, cols], op=ALU.subtract
             )
 
-        def weigh(c):
-            cols = slice(c * CHUNK, (c + 1) * CHUNK)
+        def weigh(i):
+            cols = pieces[i]
             nc.vector.scalar_tensor_tensor(
                 out=weighed[:, cols], in0=th[:, cols], scalar=1.0, in1=diff[:, cols], op0=ALU.add, op1=ALU.mult
             )
 
-        def add_back(c):
-            cols = slice(c * CHUNK, (c + 1) * CHUNK)
+        def add_back(i):
+            cols = pieces[i]
             nc.vector.scalar_tensor_tensor(
                 out=result[:, cols], in0=weighed[:, cols], scalar=0.5, in1=value[:, cols], op0=ALU.mult, op1=ALU.add
             )
             nc.sync.dma_start(out=out[:, cols], in_=result[:, cols])
 
-        turned = keep.tile([P, SUMMED_ON_TENSOR * CHUNK], F32, name="turned")
-        sums = []
-
-        def open_sums(c):
-            for b in range(c * BLOCKS, (c + 1) * BLOCKS):
+        def sum_turned(i):
+            for b in range(pieces[i].start // P, pieces[i].stop // P):
+                block = slice(b * P, (b + 1) * P)
                 acc = psum.tile([P, P], F32, name="sum%d" % b, tag="bank%d" % b)
-                for first in (True, False):
+                terms = (value, value, weighed)
+                for t, term in enumerate(terms):
                     nc.tensor.matmul(
-                        acc[:], lhsT=value[:, b * P : (b + 1) * P], rhs=identity[:],
-                        is_transpose=True, start=first, stop=False,
+                        acc[:], lhsT=term[:, block], rhs=identity[:],
+                        is_transpose=True, start=t == 0, stop=t == len(terms) - 1,
                     )
-                sums.append(acc)
+                nc.scalar.activation(out=turned[:, block], in_=acc[:], func=ACT.Copy)
 
-        def close_sums(c):
-            for b in range(c * BLOCKS, (c + 1) * BLOCKS):
-                nc.tensor.matmul(
-                    sums[b][:], lhsT=weighed[:, b * P : (b + 1) * P], rhs=identity[:],
-                    is_transpose=True, start=False, stop=True,
-                )
-                nc.scalar.activation(out=turned[:, b * P : (b + 1) * P], in_=sums[b][:], func=ACT.Copy)
-
-        def turn_back(c):
-            cols = slice(c * CHUNK, (c + 1) * CHUNK)
-            back = psum.tile([P, CHUNK], F32, name="back%d" % c, tag="bank%d" % (SUMMED_ON_TENSOR * BLOCKS + c))
-            for i in range(BLOCKS):
-                b = c * BLOCKS + i
-                nc.tensor.transpose(back[:, i * P : (i + 1) * P], turned[:, b * P : (b + 1) * P], identity[:])
+        def turn_back(i):
+            cols = pieces[i]
+            back = psum.tile(
+                [P, cols.stop - cols.start], F32, name="back%d" % i, tag="bank%d" % (sum(EARLY_WIDTHS) // P + i)
+            )
+            for c in range(cols.start, cols.stop, P):
+                nc.tensor.transpose(back[:, c - cols.start : c - cols.start + P], turned[:, c : c + P], identity[:])
             nc.scalar.activation(out=result[:, cols], in_=back[:], func=ACT.Copy, scale=0.5)
             nc.scalar.dma_start(out=out[:, cols], in_=result[:, cols])
 
         differ(0)
         differ(1)
         weigh(0)
-        open_sums(0)
-        close_sums(0)
+        sum_turned(0)
         weigh(1)
-        open_sums(1)
+        sum_turned(1)
         turn_back(0)
-        close_sums(1)
         turn_back(1)
         differ(2)
         differ(3)
         weigh(2)
         weigh(3)
         add_back(2)
+        weigh(4)
         add_back(3)
+        add_back(4)

@@ -90,6 +90,7 @@ def tile_picked_highway_gelu_p_kernel(tc, x_words, x_scales, res, w1, w2, offs, 
 
         th = keep.tile([P, S], F32, name="th")
         value = keep.tile([P, S], F32, name="value")
+        doubled = keep.tile([P, sum(EARLY_WIDTHS)], F32, name="doubled")
         gate_sums = []
         for c in range(CHUNKS):
             cols = slice(c * CHUNK, (c + 1) * CHUNK)
@@ -97,6 +98,11 @@ def tile_picked_highway_gelu_p_kernel(tc, x_words, x_scales, res, w1, w2, offs, 
             gate_sums.append(product(w2_mx, x_codes[c], c, "gate_sum", 2 * c + 1))
             nc.scalar.activation(out=value[:, cols], in_=value_sum[:], func=ACT.Gelu_apprx_tanh)
             nc.scalar.activation(out=th[:, cols], in_=gate_sums[c][:], func=ACT.Tanh, scale=-0.5)
+            if cols.stop == sum(EARLY_WIDTHS):
+                for c0 in range(0, cols.stop, CHUNK):
+                    nc.scalar.activation(
+                        out=doubled[:, c0 : c0 + CHUNK], in_=value[:, c0 : c0 + CHUNK], func=ACT.Copy, scale=2.0
+                    )
 
         diff = keep.tile([P, S], F32, name="diff")
         weighed = keep.tile([P, S], F32, name="weighed")
@@ -131,7 +137,7 @@ def tile_picked_highway_gelu_p_kernel(tc, x_words, x_scales, res, w1, w2, offs, 
             for b in range(pieces[i].start // P, pieces[i].stop // P):
                 block = slice(b * P, (b + 1) * P)
                 acc = psum.tile([P, P], F32, name="sum%d" % b, tag="bank%d" % b)
-                terms = (value, value, weighed)
+                terms = (doubled, weighed)
                 for t, term in enumerate(terms):
                     nc.tensor.matmul(
                         acc[:], lhsT=term[:, block], rhs=identity[:],

@@ -31,7 +31,6 @@ def tile_picked_highway_gelu_p_kernel(tc, x_words, x_scales, res, w1, w2, offs, 
         psum = ctx.enter_context(tc.psum_pool(name="psum", bufs=1))
 
         offsets = keep.tile([P, S // 16], U16, name="offsets")
-        nc.sync.dma_start(offsets[:], offs)
 
         scale_table = keep.tile([P, T], U8, name="scale_table", align_bytes=64)
         nc.vector.memset(scale_table[:].bitcast(I32), 0)
@@ -41,6 +40,7 @@ def tile_picked_highway_gelu_p_kernel(tc, x_words, x_scales, res, w1, w2, offs, 
 
         w2_raw = keep.tile([P, PACK, N], F32, name="w2_raw")
         nc.sync.dma_start(out=w2_raw[:], in_=w2.rearrange("(p j) n -> p j n", j=PACK))
+        nc.sync.dma_start(offsets[:], offs)
         for i in range(4):
             nc.sync.dma_start(
                 out=scale_table[i:P:32, :].bitcast(I32),

@@ -20,8 +20,7 @@ P = 128
 PACK = 4
 CHUNK = 256
 CHUNKS = S // CHUNK
-EARLY_WIDTHS = (256, 256,)
-LATE_WIDTHS = (256, 128, 128,)
+EARLY = 512
 
 
 def tile_picked_highway_gelu_p_kernel(tc, x_words, x_scales, res, w1, w2, offs, out):
@@ -67,107 +66,106 @@ def tile_picked_highway_gelu_p_kernel(tc, x_words, x_scales, res, w1, w2, offs, 
         w2_mx = (w_codes[:, :N], w_scales[:, :N])
         w1_mx = (w_codes[:, N:], w_scales[:, N:])
 
-        def product(weights, x_codes, c, label, bank):
+        th = keep.tile([P, S], F32, name="th")
+        value = keep.tile([P, S], F32, name="value")
+        doubled = keep.tile([P, EARLY], F32, name="doubled")
+        diff = keep.tile([P, S], F32, name="diff")
+        weighed = keep.tile([P, S], F32, name="weighed")
+        result = keep.tile([P, S], F32, name="result")
+        turned = keep.tile([P, EARLY], F32, name="turned")
+
+        def listed(a, b):
+            return offsets[:, a // 16 : b // 16]
+
+        x_codes = {}
+
+        def gather_words(a, b):
+            codes = keep.tile([P, b - a], U32, name="x_codes%d" % a, align_bytes=64)
+            nc.vector.tensor_copy(out=codes[:], in_=word_table[:].bitcast(U32).indirect(listed(a, b)))
+            x_codes[a] = codes
+
+        def product(weights, a, b, label, bank):
             codes, scales = weights
-            acc = psum.tile([P, CHUNK], F32, name=label + "%d" % c, tag="bank%d" % bank)
+            acc = psum.tile([P, b - a], F32, name=label + "%d" % a, tag="bank%d" % bank)
             nc.tensor.matmul_mx(
                 out=acc[:],
                 lhsT=codes.bitcast(FP8X4),
                 lhsT_scale=scales,
-                rhs=x_codes[:].bitcast(FP8X4),
-                rhs_scale=x_scale[:, c * CHUNK : (c + 1) * CHUNK],
+                rhs=x_codes[a][:].bitcast(FP8X4),
+                rhs_scale=x_scale[:, a:b],
                 start=True,
                 stop=True,
             )
             return acc
 
-        x_codes = []
-        for c in range(CHUNKS):
-            codes = keep.tile([P, CHUNK], U32, name="x_codes%d" % c, align_bytes=64)
-            picked = offsets[:, c * CHUNK // 16 : (c + 1) * CHUNK // 16]
-            nc.vector.tensor_copy(out=codes[:], in_=word_table[:].bitcast(U32).indirect(picked))
-            x_codes.append(codes)
+        def layer(a, b, bank):
+            acc = product(w1_mx, a, b, "value_sum", bank)
+            nc.scalar.activation(out=value[:, a:b], in_=acc[:], func=ACT.Gelu_apprx_tanh)
 
-        th = keep.tile([P, S], F32, name="th")
-        value = keep.tile([P, S], F32, name="value")
-        doubled = keep.tile([P, sum(EARLY_WIDTHS)], F32, name="doubled")
-        gate_sums = []
-        for c in range(CHUNKS):
-            cols = slice(c * CHUNK, (c + 1) * CHUNK)
-            value_sum = product(w1_mx, x_codes[c], c, "value_sum", 2 * c)
-            gate_sums.append(product(w2_mx, x_codes[c], c, "gate_sum", 2 * c + 1))
-            nc.scalar.activation(out=value[:, cols], in_=value_sum[:], func=ACT.Gelu_apprx_tanh)
-            nc.scalar.activation(out=th[:, cols], in_=gate_sums[c][:], func=ACT.Tanh, scale=-0.5)
-            if cols.stop == sum(EARLY_WIDTHS):
-                for c0 in range(0, cols.stop, CHUNK):
-                    nc.scalar.activation(
-                        out=doubled[:, c0 : c0 + CHUNK], in_=value[:, c0 : c0 + CHUNK], func=ACT.Copy, scale=2.0
-                    )
+        def gate(a, b, bank):
+            acc = product(w2_mx, a, b, "gate_sum", bank)
+            nc.scalar.activation(out=th[:, a:b], in_=acc[:], func=ACT.Tanh, scale=-0.5)
 
-        diff = keep.tile([P, S], F32, name="diff")
-        weighed = keep.tile([P, S], F32, name="weighed")
-        result = keep.tile([P, S], F32, name="result")
-        turned = keep.tile([P, sum(EARLY_WIDTHS)], F32, name="turned")
-        pieces = []
-        for width in EARLY_WIDTHS + LATE_WIDTHS:
-            start = pieces[-1].stop if pieces else 0
-            pieces.append(slice(start, start + width))
+        def double(a, b):
+            nc.scalar.activation(out=doubled[:, a:b], in_=value[:, a:b], func=ACT.Copy, scale=2.0)
 
-        def differ(c):
-            cols = slice(c * CHUNK, (c + 1) * CHUNK)
-            picked = offsets[:, cols.start // 16 : cols.stop // 16]
+        def differ(a, b):
             nc.vector.tensor_tensor(
-                out=diff[:, cols], in0=res_table[:].indirect(picked), in1=value[:, cols], op=ALU.subtract
+                out=diff[:, a:b], in0=res_table[:].indirect(listed(a, b)), in1=value[:, a:b], op=ALU.subtract
             )
 
-        def weigh(i):
-            cols = pieces[i]
+        def weigh(a, b):
             nc.vector.scalar_tensor_tensor(
-                out=weighed[:, cols], in0=th[:, cols], scalar=1.0, in1=diff[:, cols], op0=ALU.add, op1=ALU.mult
+                out=weighed[:, a:b], in0=th[:, a:b], scalar=1.0, in1=diff[:, a:b], op0=ALU.add, op1=ALU.mult
             )
 
-        def add_back(i):
-            cols = pieces[i]
+        def add_back(a, b, queue):
             nc.vector.scalar_tensor_tensor(
-                out=result[:, cols], in0=weighed[:, cols], scalar=0.5, in1=value[:, cols], op0=ALU.mult, op1=ALU.add
+                out=result[:, a:b], in0=weighed[:, a:b], scalar=0.5, in1=value[:, a:b], op0=ALU.mult, op1=ALU.add
             )
-            nc.sync.dma_start(out=out[:, cols], in_=result[:, cols])
+            queue.dma_start(out=out[:, a:b], in_=result[:, a:b])
 
-        def sum_turned(i):
-            for b in range(pieces[i].start // P, pieces[i].stop // P):
-                block = slice(b * P, (b + 1) * P)
-                acc = psum.tile([P, P], F32, name="sum%d" % b, tag="bank%d" % b)
-                terms = (doubled, weighed)
-                for t, term in enumerate(terms):
-                    nc.tensor.matmul(
-                        acc[:], lhsT=term[:, block], rhs=identity[:],
-                        is_transpose=True, start=t == 0, stop=t == len(terms) - 1,
-                    )
-                nc.scalar.activation(out=turned[:, block], in_=acc[:], func=ACT.Copy)
+        def sum_turned(a, b, bank):
+            acc = psum.tile([P, b - a], F32, name="sum%d" % a, tag="bank%d" % bank)
+            steps = [(term, c) for term in (doubled, weighed) for c in range(a, b, P)]
+            for k, (term, c) in enumerate(steps):
+                nc.tensor.matmul(
+                    acc[:, c - a : c - a + P], lhsT=term[:, c : c + P], rhs=identity[:],
+                    is_transpose=True, start=k == 0, stop=k == len(steps) - 1,
+                )
+            nc.scalar.activation(out=turned[:, a:b], in_=acc[:], func=ACT.Copy)
 
-        def turn_back(i):
-            cols = pieces[i]
-            back = psum.tile(
-                [P, cols.stop - cols.start], F32, name="back%d" % i, tag="bank%d" % (sum(EARLY_WIDTHS) // P + i)
-            )
-            for c in range(cols.start, cols.stop, P):
-                nc.tensor.transpose(back[:, c - cols.start : c - cols.start + P], turned[:, c : c + P], identity[:])
-            nc.scalar.activation(out=result[:, cols], in_=back[:], func=ACT.Copy, scale=0.5)
-            nc.scalar.dma_start(out=out[:, cols], in_=result[:, cols])
+        def turn_back(a, b, bank, queue):
+            back = psum.tile([P, b - a], F32, name="back%d" % a, tag="bank%d" % bank)
+            for c in range(a, b, P):
+                nc.tensor.transpose(back[:, c - a : c - a + P], turned[:, c : c + P], identity[:])
+            nc.scalar.activation(out=result[:, a:b], in_=back[:], func=ACT.Copy, scale=0.5)
+            queue.dma_start(out=out[:, a:b], in_=result[:, a:b])
 
-        differ(0)
-        differ(1)
-        weigh(0)
-        sum_turned(0)
-        weigh(1)
-        sum_turned(1)
-        turn_back(0)
-        turn_back(1)
-        differ(2)
-        differ(3)
-        weigh(2)
-        weigh(3)
-        add_back(2)
-        weigh(4)
-        add_back(3)
-        add_back(4)
+        gather_words(0, 256)
+        gather_words(256, 512)
+        gather_words(512, 1024)
+        layer(0, 256, 0)
+        gate(0, 256, 1)
+        layer(256, 512, 2)
+        gate(256, 512, 3)
+        double(0, 512)
+        layer(512, 1024, 4)
+        gate(512, 1024, 5)
+        differ(0, 256)
+        differ(256, 512)
+        weigh(0, 256)
+        sum_turned(0, 128, 0)
+        sum_turned(128, 256, 1)
+        weigh(256, 512)
+        sum_turned(256, 384, 2)
+        sum_turned(384, 512, 3)
+        turn_back(0, 256, 6, nc.scalar)
+        turn_back(256, 512, 7, nc.scalar)
+        differ(512, 768)
+        differ(768, 1024)
+        weigh(512, 768)
+        weigh(768, 1024)
+        add_back(512, 768, nc.sync)
+        add_back(768, 896, nc.sync)
+        add_back(896, 1024, nc.sync)

@@ -1,7 +1,6 @@
 from contextlib import ExitStack
 
 import concourse.mybir as mybir
-from concourse.masks import make_identity
 
 K, T, S, N = 512, 2048, 1024, 128
 FLOPS = 2 * 2 * K * S * N
@@ -18,9 +17,6 @@ ALU = mybir.AluOpType
 
 P = 128
 PACK = 4
-CHUNK = 256
-CHUNKS = S // CHUNK
-EARLY = 512
 
 
 def tile_picked_highway_gelu_p_kernel(tc, x_words, x_scales, res, w1, w2, offs, out):
@@ -30,68 +26,74 @@ def tile_picked_highway_gelu_p_kernel(tc, x_words, x_scales, res, w1, w2, offs, 
         psum = ctx.enter_context(tc.psum_pool(name="psum", bufs=1))
 
         offsets = keep.tile([P, S // 16], U16, name="offsets")
-
         scale_table = keep.tile([P, T], U8, name="scale_table", align_bytes=64)
         nc.vector.memset(scale_table[:].bitcast(I32), 0)
-        identity = keep.tile([P, P], F32, name="identity")
-        nc.vector.memset(identity[:], 0.0)
-        make_identity(nc, identity[:], nomemset=True)
 
-        w2_raw = keep.tile([P, PACK, N], F32, name="w2_raw")
-        nc.sync.dma_start(out=w2_raw[:], in_=w2.rearrange("(p j) n -> p j n", j=PACK))
+        w1_raw = keep.tile([P, PACK, N], F32, name="w1_raw")
+        nc.sync.dma_start(out=w1_raw[:], in_=w1.rearrange("(p j) n -> p j n", j=PACK))
         nc.sync.dma_start(offsets[:], offs)
         for i in range(4):
             nc.sync.dma_start(
                 out=scale_table[i:P:32, :].bitcast(I32),
                 in_=x_scales[0, i:16:4, :].bitcast(I32),
             )
-        w1_raw = keep.tile([P, PACK, N], F32, name="w1_raw")
-        nc.sync.dma_start(out=w1_raw[:], in_=w1.rearrange("(p j) n -> p j n", j=PACK))
         word_table = keep.tile([P, T], I32, name="word_table", align_bytes=64)
         nc.sync.dma_start(out=word_table[:], in_=x_words[0].rearrange("p n t -> p (n t)").bitcast(I32))
+        w2_raw = keep.tile([P, PACK, N], F32, name="w2_raw", tag="w2_bytes", align_bytes=64)
+        nc.sync.dma_start(out=w2_raw[:], in_=w2.rearrange("(p j) n -> p j n", j=PACK))
         res_table = keep.tile([P, T], F32, name="res_table", align_bytes=64)
         nc.sync.dma_start(out=res_table[:], in_=res)
-
-        x_scale = keep.tile([P, S], U8, name="x_scale", align_bytes=64)
-        nc.vector.tensor_copy(out=x_scale[:], in_=scale_table[:].indirect(offsets[:]))
-
-        grouped = keep.tile([P, 2, N, PACK], BF16, name="grouped", align_bytes=64)
-        for slot, raw in enumerate((w2_raw, w1_raw)):
-            nc.scalar.copy(out=grouped[:, slot], in_=raw[:].rearrange("p j n -> p n j"))
-        w_codes = keep.tile([P, 2 * N], U32, name="w_codes", align_bytes=64)
-        w_scales = keep.tile([P, 2 * N], U8, name="w_scales", align_bytes=64)
-        nc.vector.quantize_mx(
-            out=w_codes[:].bitcast(FP8X4), scales=w_scales[:], in_=grouped[:].rearrange("p s n j -> p (s n j)")
-        )
-        w2_mx = (w_codes[:, :N], w_scales[:, :N])
-        w1_mx = (w_codes[:, N:], w_scales[:, N:])
-
-        th = keep.tile([P, S], F32, name="th")
-        value = keep.tile([P, S], F32, name="value")
-        doubled = keep.tile([P, EARLY], F32, name="doubled")
-        diff = keep.tile([P, S], F32, name="diff")
-        weighed = keep.tile([P, S], F32, name="weighed")
-        result = keep.tile([P, S], F32, name="result")
-        turned = keep.tile([P, EARLY], F32, name="turned")
 
         def listed(a, b):
             return offsets[:, a // 16 : b // 16]
 
-        x_codes = {}
+        def round_weight(engine, raw, label):
+            grouped = keep.tile([P, N, PACK], BF16, name=label + "_grouped", align_bytes=64)
+            engine.tensor_copy(out=grouped[:], in_=raw[:].rearrange("p j n -> p n j"))
+            return grouped
 
-        def gather_words(a, b):
-            codes = keep.tile([P, b - a], U32, name="x_codes%d" % a, align_bytes=64)
-            nc.vector.tensor_copy(out=codes[:], in_=word_table[:].bitcast(U32).indirect(listed(a, b)))
-            x_codes[a] = codes
+        def quantise(grouped, label):
+            codes = keep.tile([P, N], U32, name=label + "_codes", align_bytes=64)
+            scales = keep.tile([P, N], U8, name=label + "_scales", align_bytes=64)
+            nc.vector.quantize_mx(
+                out=codes[:].bitcast(FP8X4), scales=scales[:], in_=grouped[:].rearrange("p n j -> p (n j)")
+            )
+            return codes, scales
+
+        w1_mx = quantise(round_weight(nc.vector, w1_raw, "w1"), "w1")
+        x_scale = keep.tile([P, S], U8, name="x_scale", align_bytes=64)
+        nc.vector.tensor_copy(out=x_scale[:], in_=scale_table[:].indirect(offsets[:]))
+        w2_grouped = round_weight(nc.gpsimd, w2_raw, "w2")
+
+        def gather_words(codes, base, a, b):
+            nc.vector.tensor_copy(
+                out=codes[:, a - base : b - base], in_=word_table[:].bitcast(U32).indirect(listed(a, b))
+            )
+
+        early_codes = keep.tile([P, 512], U32, name="early_codes", align_bytes=64)
+        gather_words(early_codes, 0, 0, 256)
+        gather_words(early_codes, 0, 256, 512)
+        w2_mx = quantise(w2_grouped, "w2")
+        late_codes = keep.tile([P, 512], U32, name="late_codes", tag="w2_bytes", align_bytes=64)
+        gather_words(late_codes, 512, 512, 768)
+        gather_words(late_codes, 512, 768, 1024)
+
+        th = keep.tile([P, S], F32, name="th")
+        value = keep.tile([P, S], F32, name="value")
+        carried = keep.tile([P, S], F32, name="carried")
+        first = keep.tile([P, S], F32, name="first")
+        second = keep.tile([P, S], F32, name="second")
+        result = keep.tile([P, S], F32, name="result")
 
         def product(weights, a, b, label, bank):
             codes, scales = weights
+            picked = early_codes[:, a:b] if a < 512 else late_codes[:, a - 512 : b - 512]
             acc = psum.tile([P, b - a], F32, name=label + "%d" % a, tag="bank%d" % bank)
             nc.tensor.matmul_mx(
                 out=acc[:],
-                lhsT=codes.bitcast(FP8X4),
-                lhsT_scale=scales,
-                rhs=x_codes[a][:].bitcast(FP8X4),
+                lhsT=codes[:].bitcast(FP8X4),
+                lhsT_scale=scales[:],
+                rhs=picked.bitcast(FP8X4),
                 rhs_scale=x_scale[:, a:b],
                 start=True,
                 stop=True,
@@ -104,68 +106,67 @@ def tile_picked_highway_gelu_p_kernel(tc, x_words, x_scales, res, w1, w2, offs, 
 
         def gate(a, b, bank):
             acc = product(w2_mx, a, b, "gate_sum", bank)
-            nc.scalar.activation(out=th[:, a:b], in_=acc[:], func=ACT.Tanh, scale=-0.5)
+            nc.scalar.activation(out=th[:, a:b], in_=acc[:], func=ACT.Tanh, scale=0.5)
 
-        def double(a, b):
-            nc.scalar.activation(out=doubled[:, a:b], in_=value[:, a:b], func=ACT.Copy, scale=2.0)
+        def fetch(a, b):
+            nc.scalar.activation(
+                out=carried[:, a:b], in_=res_table[:].indirect(listed(a, b)), func=ACT.Copy, scale=0.5
+            )
 
-        def differ(a, b):
+        def fetch_differ(a, b):
             nc.vector.tensor_tensor(
-                out=diff[:, a:b], in0=res_table[:].indirect(listed(a, b)), in1=value[:, a:b], op=ALU.subtract
+                out=first[:, a:b], in0=res_table[:].indirect(listed(a, b)), in1=value[:, a:b], op=ALU.subtract
             )
 
-        def weigh(a, b):
+        def weigh_difference(a, b):
             nc.vector.scalar_tensor_tensor(
-                out=weighed[:, a:b], in0=th[:, a:b], scalar=1.0, in1=diff[:, a:b], op0=ALU.add, op1=ALU.mult
+                out=second[:, a:b], in0=th[:, a:b], scalar=-1.0, in1=first[:, a:b], op0=ALU.add, op1=ALU.mult
             )
 
-        def add_back(a, b, queue):
+        def add_back(a, b):
             nc.vector.scalar_tensor_tensor(
-                out=result[:, a:b], in0=weighed[:, a:b], scalar=0.5, in1=value[:, a:b], op0=ALU.mult, op1=ALU.add
+                out=result[:, a:b], in0=second[:, a:b], scalar=-0.5, in1=value[:, a:b], op0=ALU.mult, op1=ALU.add
             )
-            queue.dma_start(out=out[:, a:b], in_=result[:, a:b])
+            nc.sync.dma_start(out=out[:, a:b], in_=result[:, a:b])
 
-        def sum_turned(a, b, bank):
-            acc = psum.tile([P, b - a], F32, name="sum%d" % a, tag="bank%d" % bank)
-            steps = [(term, c) for term in (doubled, weighed) for c in range(a, b, P)]
-            for k, (term, c) in enumerate(steps):
-                nc.tensor.matmul(
-                    acc[:, c - a : c - a + P], lhsT=term[:, c : c + P], rhs=identity[:],
-                    is_transpose=True, start=k == 0, stop=k == len(steps) - 1,
-                )
-            nc.scalar.activation(out=turned[:, a:b], in_=acc[:], func=ACT.Copy)
+        def weigh_value(a, b):
+            nc.vector.scalar_tensor_tensor(
+                out=first[:, a:b], in0=th[:, a:b], scalar=1.0, in1=value[:, a:b], op0=ALU.add, op1=ALU.mult
+            )
 
-        def turn_back(a, b, bank, queue):
-            back = psum.tile([P, b - a], F32, name="back%d" % a, tag="bank%d" % bank)
-            for c in range(a, b, P):
-                nc.tensor.transpose(back[:, c - a : c - a + P], turned[:, c : c + P], identity[:])
-            nc.scalar.activation(out=result[:, a:b], in_=back[:], func=ACT.Copy, scale=0.5)
-            queue.dma_start(out=out[:, a:b], in_=result[:, a:b])
+        def weigh_carried(a, b):
+            nc.vector.scalar_tensor_tensor(
+                out=second[:, a:b], in0=th[:, a:b], scalar=-1.0, in1=carried[:, a:b], op0=ALU.add, op1=ALU.mult
+            )
 
-        gather_words(0, 256)
-        gather_words(256, 512)
-        gather_words(512, 1024)
+        def join(a, b):
+            nc.vector.scalar_tensor_tensor(
+                out=result[:, a:b], in0=first[:, a:b], scalar=0.5, in1=second[:, a:b], op0=ALU.mult, op1=ALU.subtract
+            )
+            nc.sync.dma_start(out=out[:, a:b], in_=result[:, a:b])
+
         layer(0, 256, 0)
-        gate(0, 256, 1)
-        layer(256, 512, 2)
+        layer(256, 512, 1)
+        gate(0, 256, 2)
         gate(256, 512, 3)
-        double(0, 512)
-        layer(512, 1024, 4)
-        gate(512, 1024, 5)
-        differ(0, 256)
-        differ(256, 512)
-        weigh(0, 256)
-        sum_turned(0, 128, 0)
-        sum_turned(128, 256, 1)
-        weigh(256, 512)
-        sum_turned(256, 384, 2)
-        sum_turned(384, 512, 3)
-        turn_back(0, 256, 6, nc.scalar)
-        turn_back(256, 512, 7, nc.scalar)
-        differ(512, 768)
-        differ(768, 1024)
-        weigh(512, 768)
-        weigh(768, 1024)
-        add_back(512, 768, nc.sync)
-        add_back(768, 896, nc.sync)
-        add_back(896, 1024, nc.sync)
+        fetch(256, 512)
+        layer(512, 768, 4)
+        gate(512, 768, 5)
+        fetch(512, 768)
+        layer(768, 1024, 6)
+        gate(768, 1024, 7)
+        fetch(768, 1024)
+        fetch_differ(0, 256)
+        weigh_value(256, 512)
+        weigh_difference(0, 256)
+        weigh_carried(256, 512)
+        add_back(0, 256)
+        join(256, 512)
+        weigh_value(512, 768)
+        weigh_carried(512, 768)
+        weigh_value(768, 1024)
+        join(512, 768)
+        weigh_carried(768, 896)
+        weigh_carried(896, 1024)
+        join(768, 896)
+        join(896, 1024)

@@ -63,6 +63,8 @@ def tile_picked_highway_gelu_p_kernel(tc, x_words, x_scales, res, w1, w2, offs, 
         w1_mx = quantise(round_weight(nc.vector, w1_raw, "w1"), "w1")
         x_scale = keep.tile([P, S], U8, name="x_scale", align_bytes=64)
         nc.vector.tensor_copy(out=x_scale[:], in_=scale_table[:].indirect(offsets[:]))
+        spare = keep.tile([P, N, PACK], BF16, name="spare", tag="w1_grouped", align_bytes=64)
+        nc.gpsimd.tensor_copy(out=spare[:], in_=w1_raw[:].rearrange("p j n -> p n j"))
         w2_grouped = round_weight(nc.gpsimd, w2_raw, "w2")
 
         def gather_words(codes, base, a, b):

from contextlib import ExitStack

import concourse.mybir as mybir

K, T, S, N = 512, 2048, 1024, 128
FLOPS = 2 * 2 * K * S * N

F32 = mybir.dt.float32
BF16 = mybir.dt.bfloat16
I32 = mybir.dt.int32
U32 = mybir.dt.uint32
U16 = mybir.dt.uint16
U8 = mybir.dt.uint8
FP8X4 = mybir.dt.float8_e4m3fn_x4
ACT = mybir.ActivationFunctionType
ALU = mybir.AluOpType

P = 128
PACK = 4


def tile_picked_highway_gelu_p_kernel(tc, x_words, x_scales, res, w1, w2, offs, out):
    nc = tc.nc
    with ExitStack() as ctx:
        keep = ctx.enter_context(tc.tile_pool(name="keep", bufs=1))
        psum = ctx.enter_context(tc.psum_pool(name="psum", bufs=1))

        offsets = keep.tile([P, S // 16], U16, name="offsets")
        scale_table = keep.tile([P, T], U8, name="scale_table", align_bytes=64)
        nc.vector.memset(scale_table[:].bitcast(I32), 0)

        w1_raw = keep.tile([P, PACK, N], F32, name="w1_raw")
        nc.sync.dma_start(out=w1_raw[:], in_=w1.rearrange("(p j) n -> p j n", j=PACK))
        nc.sync.dma_start(offsets[:], offs)
        for i in range(4):
            nc.sync.dma_start(
                out=scale_table[i:P:32, :].bitcast(I32),
                in_=x_scales[0, i:16:4, :].bitcast(I32),
            )
        word_table = keep.tile([P, T], I32, name="word_table", align_bytes=64)
        nc.sync.dma_start(out=word_table[:], in_=x_words[0].rearrange("p n t -> p (n t)").bitcast(I32))
        w2_raw = keep.tile([P, PACK, N], F32, name="w2_raw", tag="w2_bytes", align_bytes=64)
        nc.sync.dma_start(out=w2_raw[:], in_=w2.rearrange("(p j) n -> p j n", j=PACK))
        res_table = keep.tile([P, T], F32, name="res_table", align_bytes=64)
        nc.sync.dma_start(out=res_table[:], in_=res)

        def listed(a, b):
            return offsets[:, a // 16 : b // 16]

        def round_weight(engine, raw, label):
            grouped = keep.tile([P, N, PACK], BF16, name=label + "_grouped", align_bytes=64)
            engine.tensor_copy(out=grouped[:], in_=raw[:].rearrange("p j n -> p n j"))
            return grouped

        def quantise(grouped, label):
            codes = keep.tile([P, N], U32, name=label + "_codes", align_bytes=64)
            scales = keep.tile([P, N], U8, name=label + "_scales", align_bytes=64)
            nc.vector.quantize_mx(
                out=codes[:].bitcast(FP8X4), scales=scales[:], in_=grouped[:].rearrange("p n j -> p (n j)")
            )
            return codes, scales

        w1_mx = quantise(round_weight(nc.vector, w1_raw, "w1"), "w1")
        x_scale = keep.tile([P, S], U8, name="x_scale", align_bytes=64)
        nc.vector.tensor_copy(out=x_scale[:], in_=scale_table[:].indirect(offsets[:]))
        spare = keep.tile([P, N, PACK], BF16, name="spare", tag="w1_grouped", align_bytes=64)
        nc.gpsimd.tensor_copy(out=spare[:], in_=w1_raw[:].rearrange("p j n -> p n j"))
        w2_grouped = round_weight(nc.gpsimd, w2_raw, "w2")

        def gather_words(codes, base, a, b):
            nc.vector.tensor_copy(
                out=codes[:, a - base : b - base], in_=word_table[:].bitcast(U32).indirect(listed(a, b))
            )

        early_codes = keep.tile([P, 512], U32, name="early_codes", align_bytes=64)
        gather_words(early_codes, 0, 0, 256)
        gather_words(early_codes, 0, 256, 512)
        w2_mx = quantise(w2_grouped, "w2")
        late_codes = keep.tile([P, 512], U32, name="late_codes", tag="w2_bytes", align_bytes=64)
        gather_words(late_codes, 512, 512, 768)
        gather_words(late_codes, 512, 768, 1024)

        th = keep.tile([P, S], F32, name="th")
        value = keep.tile([P, S], F32, name="value")
        carried = keep.tile([P, S], F32, name="carried")
        first = keep.tile([P, S], F32, name="first")
        second = keep.tile([P, S], F32, name="second")
        result = keep.tile([P, S], F32, name="result")

        def product(weights, a, b, label, bank):
            codes, scales = weights
            picked = early_codes[:, a:b] if a < 512 else late_codes[:, a - 512 : b - 512]
            acc = psum.tile([P, b - a], F32, name=label + "%d" % a, tag="bank%d" % bank)
            nc.tensor.matmul_mx(
                out=acc[:],
                lhsT=codes[:].bitcast(FP8X4),
                lhsT_scale=scales[:],
                rhs=picked.bitcast(FP8X4),
                rhs_scale=x_scale[:, a:b],
                start=True,
                stop=True,
            )
            return acc

        def layer(a, b, bank):
            acc = product(w1_mx, a, b, "value_sum", bank)
            nc.scalar.activation(out=value[:, a:b], in_=acc[:], func=ACT.Gelu_apprx_tanh)

        def gate(a, b, bank):
            acc = product(w2_mx, a, b, "gate_sum", bank)
            nc.scalar.activation(out=th[:, a:b], in_=acc[:], func=ACT.Tanh, scale=0.5)

        def fetch(a, b):
            nc.scalar.activation(
                out=carried[:, a:b], in_=res_table[:].indirect(listed(a, b)), func=ACT.Copy, scale=0.5
            )

        def fetch_differ(a, b):
            nc.vector.tensor_tensor(
                out=first[:, a:b], in0=res_table[:].indirect(listed(a, b)), in1=value[:, a:b], op=ALU.subtract
            )

        def weigh_difference(a, b):
            nc.vector.scalar_tensor_tensor(
                out=second[:, a:b], in0=th[:, a:b], scalar=-1.0, in1=first[:, a:b], op0=ALU.add, op1=ALU.mult
            )

        def add_back(a, b):
            nc.vector.scalar_tensor_tensor(
                out=result[:, a:b], in0=second[:, a:b], scalar=-0.5, in1=value[:, a:b], op0=ALU.mult, op1=ALU.add
            )
            nc.sync.dma_start(out=out[:, a:b], in_=result[:, a:b])

        def weigh_value(a, b):
            nc.vector.scalar_tensor_tensor(
                out=first[:, a:b], in0=th[:, a:b], scalar=1.0, in1=value[:, a:b], op0=ALU.add, op1=ALU.mult
            )

        def weigh_carried(a, b):
            nc.vector.scalar_tensor_tensor(
                out=second[:, a:b], in0=th[:, a:b], scalar=-1.0, in1=carried[:, a:b], op0=ALU.add, op1=ALU.mult
            )

        def join(a, b):
            nc.vector.scalar_tensor_tensor(
                out=result[:, a:b], in0=first[:, a:b], scalar=0.5, in1=second[:, a:b], op0=ALU.mult, op1=ALU.subtract
            )
            nc.sync.dma_start(out=out[:, a:b], in_=result[:, a:b])

        layer(0, 256, 0)
        layer(256, 512, 1)
        gate(0, 256, 2)
        gate(256, 512, 3)
        fetch(256, 512)
        layer(512, 768, 4)
        gate(512, 768, 5)
        fetch(512, 768)
        layer(768, 1024, 6)
        gate(768, 1024, 7)
        fetch(768, 1024)
        fetch_differ(0, 256)
        weigh_value(256, 512)
        weigh_difference(0, 256)
        weigh_carried(256, 512)
        add_back(0, 256)
        join(256, 512)
        weigh_value(512, 768)
        weigh_carried(512, 768)
        weigh_value(768, 1024)
        join(512, 768)
        weigh_carried(768, 896)
        weigh_carried(896, 1024)
        join(768, 896)
        join(896, 1024)
